import numpy as np
import ml_dtypes


def mxq(x, axis, fmt="e4m3"):
    dtype, down = {"e4m3": (ml_dtypes.float8_e4m3fn, 7), "e5m2": (ml_dtypes.float8_e5m2, 14)}[fmt]
    v = np.moveaxis(np.asarray(x, np.float32).astype(ml_dtypes.bfloat16).astype(np.float64), axis, -1)
    blocks = v.reshape(v.shape[:-1] + (-1, 32))
    amax = np.abs(blocks).max(-1, keepdims=True)
    byte = np.maximum(np.where(amax > 0, np.frexp(amax)[1] - 1 + 127, 0) - down, 1)
    scale = np.exp2(byte - 127.0)
    codes = (blocks / scale).astype(np.float32).astype(dtype).astype(np.float64)
    return np.moveaxis((codes * scale).reshape(v.shape), -1, axis)


WIDE = False


def mx_kscale(k):
    if not WIDE:
        return np.ones(k)
    levels = np.array([10, -10, 5, -5, 0])
    if k % 512:
        return np.exp2(np.random.permutation(np.resize(levels, k // 32))).repeat(32)
    a = np.empty((k // 512, 16))
    for p in range(k // 512):
        a[p, :8] = np.random.permutation(np.resize(levels, 8))
        for g in range(8):
            far = levels[np.abs(levels - a[p, g]) >= 10]
            a[p, g + 8] = far[np.random.randint(len(far))]
    return np.exp2(a.ravel()).repeat(32)


def f64(x):
    return np.asarray(x).astype(np.float64)


def striped(idx):
    return np.tile(idx.reshape(-1, 16).T, (8, 1)).astype(np.uint16)


def unstriped(offs):
    return offs[:16].T.reshape(-1).astype(np.int64)


def pack_weight(w):
    k, n = w.shape
    w = f64(np.asarray(w, np.float32).astype(ml_dtypes.bfloat16)).reshape(k // 32, 32, n)
    amax = np.abs(w).max(1)
    byte = np.clip(np.where(amax > 0, np.frexp(amax)[1] - 1 + 127 - 7, 1), 1, 254)
    scaled = (w * np.exp2(127.0 - byte)[:, None, :]).reshape(k, n).astype(np.float32)
    words = np.ascontiguousarray(scaled.reshape(k // 512, 128, 4, n).transpose(0, 1, 3, 2)).astype(ml_dtypes.float8_e4m3fn).view(np.uint8)
    return words, np.ascontiguousarray(byte.astype(np.uint8).reshape(k // 512, 16, n))


def unpack_weight(words, scales):
    g, p, n, _ = words.shape
    vals = np.ascontiguousarray(words).view(ml_dtypes.float8_e4m3fn).astype(np.float64) * np.repeat(np.exp2(scales.astype(np.float64) - 127.0), 8, axis=1)[..., None]
    return vals.transpose(0, 1, 3, 2).reshape(g * 512, n)


K, T, D, S, V, N = 512, 4096, 4, 2048, 512, 512


def setup_inputs():
    n = np.random.standard_normal
    s = mx_kscale(K)[:, None]
    words, scales = pack_weight(n((K, N)) / np.sqrt(K) / s)
    return {
        "xT": (n((K, T)) * s).astype(np.float32),
        "w_words": words,
        "w_scales": scales,
        "b": (0.3 * n((N, 1))).astype(np.float32),
        "offs": striped(np.concatenate([np.random.permutation(T)[:V] for _ in range(D)])),
    }


def reference(xT, w_words, w_scales, b, offs):
    w = unpack_weight(w_words, w_scales)
    idx = unstriped(offs)
    x = np.empty((K, V))
    for l in range(D):
        r = l // 4 * (4 * K // D) + l % 4 + 4 * np.arange(K // D)
        x[r] = f64(xT)[r][:, idx[l * V:(l + 1) * V]]
    xq = mxq(x, 0, "e4m3")
    return (w.T @ xq) + f64(b)

@@ -1,0 +1,119 @@
+from contextlib import ExitStack
+
+import concourse.mybir as mybir
+
+K, T, LEVELS, V, M = 512, 4096, 4, 512, 512
+P = 128
+FLOPS = 2 * K * V * M
+
+F32 = mybir.dt.float32
+BF16 = mybir.dt.bfloat16
+I32 = mybir.dt.int32
+U32 = mybir.dt.uint32
+U16 = mybir.dt.uint16
+U8 = mybir.dt.uint8
+FP8X4 = mybir.dt.float8_e4m3fn_x4
+MULT = mybir.AluOpType.mult
+ADD = mybir.AluOpType.add
+IDENT = mybir.ActivationFunctionType.Identity
+
+G = 128
+PIECES = [(0, 128), (128, 128), (256, 256)]
+
+
+def tile_picked_grid_lin_bias_sub_l_kernel(tc, xT, w_words, w_scales, b, offs, out):
+    nc = tc.nc
+    with ExitStack() as ctx:
+        keep = ctx.enter_context(tc.tile_pool(name="keep", bufs=1))
+        psum = ctx.enter_context(tc.psum_pool(name="psum", bufs=1))
+
+        offsets = keep.tile([P, LEVELS * V // 16], U16, name="offsets")
+        tables = [keep.tile([P, T], F32, name=f"table{l}") for l in range(LEVELS)]
+        w_codes = keep.tile([P, M], U32, name="w_codes", align_bytes=64)
+        w_plane = keep.tile([P, M], U8, name="w_plane", align_bytes=64)
+        bias = keep.tile([P, M // P], F32, name="bias")
+        ones = keep.tile([P, G], F32, name="ones")
+        warm = keep.tile([P, 8], F32, name="warm")
+        last = keep.tile([P, V], F32, name="last")
+        xb = keep.tile([P, V, LEVELS], BF16, name="xb", align_bytes=64)
+        x_codes = keep.tile([P, V], U32, name="x_codes", align_bytes=64)
+        x_plane = keep.tile([P, V], U8, name="x_plane", align_bytes=64)
+        res = keep.tile([P, M // P, V], F32, name="res")
+
+        nc.vector.memset(w_plane[:].bitcast(I32), 0)
+        nc.vector.memset(ones[:], 1.0)
+        nc.scalar.activation(warm[:, 0:1], ones[:, 0:1], IDENT, bias=ones[:, 1:2])
+
+        x_levels = xT.rearrange("(f l) t -> l f t", l=LEVELS)
+        nc.sync.dma_start(tables[0][:], x_levels[0])
+        nc.sync.dma_start(offsets[:], offs)
+        for l in range(1, LEVELS):
+            nc.sync.dma_start(tables[l][:], x_levels[l])
+        nc.sync.dma_start(w_codes[:].bitcast(I32), w_words[0].rearrange("p m t -> p (m t)").bitcast(I32))
+        for q in range(4):
+            nc.sync.dma_start(w_plane[32 * q : 32 * q + 4, :].bitcast(I32), w_scales[0, 4 * q : 4 * q + 4, :].bitcast(I32))
+        with nc.allow_non_contiguous_dma(reason="one bias value for each output row"):
+            nc.sync.dma_start(bias[:], b.rearrange("(j p) o -> p (j o)", p=P))
+
+        cols = V // 16
+        for l in range(LEVELS - 1):
+            nc.vector.tensor_copy(xb[:, :, l], tables[l][:].indirect(offsets[:, l * cols : (l + 1) * cols]))
+
+        l3 = LEVELS - 1
+
+        def gather(i):
+            c0 = l3 * cols + i * (G // 16)
+            nc.vector.tensor_tensor(last[:, i * G : (i + 1) * G], tables[l3][:].indirect(offsets[:, c0 : c0 + G // 16]), ones[:], MULT)
+
+        def cast(n):
+            v0, w = PIECES[n]
+            nc.vector.tensor_copy(xb[:, v0 : v0 + w, l3], last[:, v0 : v0 + w])
+
+        def quant(n):
+            v0, w = PIECES[n]
+            nc.vector.quantize_mx(
+                out=x_codes[:, v0 : v0 + w].bitcast(FP8X4),
+                scales=x_plane[:, v0 : v0 + w],
+                in_=xb[:, v0 : v0 + w, :].rearrange("p v l -> p (v l)"),
+            )
+
+        out_v = out.rearrange("(j p) v -> p j v", p=P)
+
+        def product(n, on_vector):
+            v0, w = PIECES[n]
+            per_bank = 256 // w
+            for h in range(4 // per_bank):
+                acc = psum.tile([P, per_bank, w], F32, name=f"acc{n}_{h}")
+                for i in range(per_bank):
+                    j = h * per_bank + i
+                    nc.tensor.matmul_mx(
+                        out=acc[:, i, :],
+                        lhsT=w_codes[:, j * P : (j + 1) * P].bitcast(FP8X4),
+                        lhsT_scale=w_plane[:, j * P : (j + 1) * P],
+                        rhs=x_codes[:, v0 : v0 + w].bitcast(FP8X4),
+                        rhs_scale=x_plane[:, v0 : v0 + w],
+                        start=True,
+                        stop=True,
+                    )
+                for i in range(per_bank):
+                    j = h * per_bank + i
+                    if h in on_vector:
+                        nc.vector.tensor_scalar(res[:, j, v0 : v0 + w], acc[:, i, :], bias[:, j : j + 1], None, ADD)
+                    else:
+                        nc.scalar.activation(res[:, j, v0 : v0 + w], acc[:, i, :], IDENT, bias=bias[:, j : j + 1])
+                js = slice(h * per_bank, (h + 1) * per_bank)
+                nc.sync.dma_start(out_v[:, js, v0 : v0 + w], res[:, js, v0 : v0 + w])
+
+        gather(0)
+        gather(1)
+        cast(0)
+        gather(2)
+        quant(0)
+        cast(1)
+        gather(3)
+        quant(1)
+        cast(2)
+        quant(2)
+        product(0, ())
+        product(1, ())
+        product(2, (1, 3))

@@ -1,6 +1,7 @@
 from contextlib import ExitStack
 
 import concourse.mybir as mybir
+from concourse.masks import make_identity
 
 K, T, LEVELS, V, M = 512, 4096, 4, 512, 512
 P = 128
@@ -18,7 +19,8 @@ ADD = mybir.AluOpType.add
 IDENT = mybir.ActivationFunctionType.Identity
 
 G = 128
-PIECES = [(0, 128), (128, 128), (256, 256)]
+WARM = 20
+SPLIT = 2048
 
 
 def tile_picked_grid_lin_bias_sub_l_kernel(tc, xT, w_words, w_scales, b, offs, out):
@@ -31,89 +33,129 @@ def tile_picked_grid_lin_bias_sub_l_kernel(tc, xT, w_words, w_scales, b, offs, o
         tables = [keep.tile([P, T], F32, name=f"table{l}") for l in range(LEVELS)]
         w_codes = keep.tile([P, M], U32, name="w_codes", align_bytes=64)
         w_plane = keep.tile([P, M], U8, name="w_plane", align_bytes=64)
+        bias_rows = keep.tile([P, P], F32, name="bias_rows")
+        ident = keep.tile([P, P], F32, name="ident")
         bias = keep.tile([P, M // P], F32, name="bias")
         ones = keep.tile([P, G], F32, name="ones")
-        warm = keep.tile([P, 8], F32, name="warm")
         last = keep.tile([P, V], F32, name="last")
         xb = keep.tile([P, V, LEVELS], BF16, name="xb", align_bytes=64)
         x_codes = keep.tile([P, V], U32, name="x_codes", align_bytes=64)
         x_plane = keep.tile([P, V], U8, name="x_plane", align_bytes=64)
         res = keep.tile([P, M // P, V], F32, name="res")
 
+        nc.vector.memset(bias_rows[:], 0.0)
         nc.vector.memset(w_plane[:].bitcast(I32), 0)
         nc.vector.memset(ones[:], 1.0)
-        nc.scalar.activation(warm[:, 0:1], ones[:, 0:1], IDENT, bias=ones[:, 1:2])
+        make_identity(nc, ident[:])
 
+        l3 = LEVELS - 1
         x_levels = xT.rearrange("(f l) t -> l f t", l=LEVELS)
         nc.sync.dma_start(tables[0][:], x_levels[0])
         nc.sync.dma_start(offsets[:], offs)
-        for l in range(1, LEVELS):
+        nc.sync.dma_start(bias_rows[0 : M // P, :], b.rearrange("(j p) o -> j (p o)", p=P))
+        for l in range(1, l3):
             nc.sync.dma_start(tables[l][:], x_levels[l])
-        nc.sync.dma_start(w_codes[:].bitcast(I32), w_words[0].rearrange("p m t -> p (m t)").bitcast(I32))
+        nc.sync.dma_start(tables[l3][:, :SPLIT], x_levels[l3][:, :SPLIT])
+        nc.sync.dma_start(tables[l3][:, SPLIT:], x_levels[l3][:, SPLIT:])
         for q in range(4):
             nc.sync.dma_start(w_plane[32 * q : 32 * q + 4, :].bitcast(I32), w_scales[0, 4 * q : 4 * q + 4, :].bitcast(I32))
-        with nc.allow_non_contiguous_dma(reason="one bias value for each output row"):
-            nc.sync.dma_start(bias[:], b.rearrange("(j p) o -> p (j o)", p=P))
+        nc.sync.dma_start(w_codes[:].bitcast(I32), w_words[0].rearrange("p m t -> p (m t)").bitcast(I32))
+
+        turned = psum.tile([P, P], F32, name="turned", tag="bank7")
+        nc.tensor.transpose(turned[:], bias_rows[:], ident[:])
+        nc.scalar.activation(bias[:], turned[:, 0 : M // P], IDENT)
+        for i in range(WARM):
+            nc.tensor.transpose(turned[:], tables[l3][:, 0:P], ident[:])
 
         cols = V // 16
-        for l in range(LEVELS - 1):
+        for l in range(l3):
             nc.vector.tensor_copy(xb[:, :, l], tables[l][:].indirect(offsets[:, l * cols : (l + 1) * cols]))
 
-        l3 = LEVELS - 1
+        def gather(n):
+            c0 = l3 * cols + n * (G // 16)
+            nc.vector.tensor_tensor(last[:, n * G : (n + 1) * G], tables[l3][:].indirect(offsets[:, c0 : c0 + G // 16]), ones[:], MULT)
 
-        def gather(i):
-            c0 = l3 * cols + i * (G // 16)
-            nc.vector.tensor_tensor(last[:, i * G : (i + 1) * G], tables[l3][:].indirect(offsets[:, c0 : c0 + G // 16]), ones[:], MULT)
-
-        def cast(n):
-            v0, w = PIECES[n]
-            nc.vector.tensor_copy(xb[:, v0 : v0 + w, l3], last[:, v0 : v0 + w])
+        def cast(n, on_vector):
+            vs = slice(n * G, (n + 1) * G)
+            if on_vector:
+                nc.vector.tensor_copy(xb[:, vs, l3], last[:, vs])
+            else:
+                nc.scalar.activation(xb[:, vs, l3], last[:, vs], IDENT)
 
         def quant(n):
-            v0, w = PIECES[n]
+            vs = slice(n * G, (n + 1) * G)
             nc.vector.quantize_mx(
-                out=x_codes[:, v0 : v0 + w].bitcast(FP8X4),
-                scales=x_plane[:, v0 : v0 + w],
-                in_=xb[:, v0 : v0 + w, :].rearrange("p v l -> p (v l)"),
+                out=x_codes[:, vs].bitcast(FP8X4),
+                scales=x_plane[:, vs],
+                in_=xb[:, vs, :].rearrange("p v l -> p (v l)"),
             )
 
         out_v = out.rearrange("(j p) v -> p j v", p=P)
+        accs = {}
 
-        def product(n, on_vector):
-            v0, w = PIECES[n]
-            per_bank = 256 // w
-            for h in range(4 // per_bank):
-                acc = psum.tile([P, per_bank, w], F32, name=f"acc{n}_{h}")
+        def product(n, banks):
+            vs = slice(n * G, (n + 1) * G)
+            per_bank = 4 // len(banks)
+            for h, bank in enumerate(banks):
+                acc = psum.tile([P, per_bank, G], F32, name=f"acc{bank}", tag=f"bank{bank}")
                 for i in range(per_bank):
                     j = h * per_bank + i
+                    accs[(n, j)] = acc[:, i, :]
                     nc.tensor.matmul_mx(
                         out=acc[:, i, :],
                         lhsT=w_codes[:, j * P : (j + 1) * P].bitcast(FP8X4),
                         lhsT_scale=w_plane[:, j * P : (j + 1) * P],
-                        rhs=x_codes[:, v0 : v0 + w].bitcast(FP8X4),
-                        rhs_scale=x_plane[:, v0 : v0 + w],
+                        rhs=x_codes[:, vs].bitcast(FP8X4),
+                        rhs_scale=x_plane[:, vs],
                         start=True,
                         stop=True,
                     )
-                for i in range(per_bank):
-                    j = h * per_bank + i
-                    if h in on_vector:
-                        nc.vector.tensor_scalar(res[:, j, v0 : v0 + w], acc[:, i, :], bias[:, j : j + 1], None, ADD)
-                    else:
-                        nc.scalar.activation(res[:, j, v0 : v0 + w], acc[:, i, :], IDENT, bias=bias[:, j : j + 1])
-                js = slice(h * per_bank, (h + 1) * per_bank)
-                nc.sync.dma_start(out_v[:, js, v0 : v0 + w], res[:, js, v0 : v0 + w])
+
+        def empty(n, j, on_vector):
+            vs = slice(n * G, (n + 1) * G)
+            if on_vector:
+                nc.vector.tensor_scalar(res[:, j, vs], accs[(n, j)], bias[:, j : j + 1], None, ADD)
+            else:
+                nc.scalar.activation(res[:, j, vs], accs[(n, j)], IDENT, bias=bias[:, j : j + 1])
+
+        def store(j0, j1, v0, v1):
+            nc.sync.dma_start(out_v[:, j0:j1, v0:v1], res[:, j0:j1, v0:v1])
 
         gather(0)
         gather(1)
-        cast(0)
+        cast(0, True)
+        cast(1, False)
         gather(2)
         quant(0)
-        cast(1)
+        cast(2, False)
         gather(3)
         quant(1)
-        cast(2)
+        cast(3, True)
         quant(2)
-        product(0, ())
-        product(1, ())
-        product(2, (1, 3))
+        quant(3)
+        product(0, (0, 1))
+        product(1, (2,))
+        product(2, (3,))
+        product(3, (4, 5, 6, 7))
+        empty(0, 0, False)
+        empty(0, 1, False)
+        store(0, 2, 0, G)
+        empty(0, 2, False)
+        empty(0, 3, False)
+        store(2, 4, 0, G)
+        empty(1, 0, False)
+        empty(1, 1, False)
+        empty(1, 2, False)
+        empty(1, 3, False)
+        empty(2, 0, True)
+        empty(2, 1, True)
+        empty(2, 2, True)
+        empty(2, 3, True)
+        empty(3, 0, False)
+        store(0, 1, G, V)
+        empty(3, 1, False)
+        store(1, 2, G, V)
+        empty(3, 2, False)
+        store(2, 3, G, V)
+        empty(3, 3, True)
+        store(3, 4, G, V)

@@ -20,7 +20,6 @@ IDENT = mybir.ActivationFunctionType.Identity
 
 G = 128
 WARM = 20
-SPLIT = 2048
 
 
 def tile_picked_grid_lin_bias_sub_l_kernel(tc, xT, w_words, w_scales, b, offs, out):
@@ -30,7 +29,11 @@ def tile_picked_grid_lin_bias_sub_l_kernel(tc, xT, w_words, w_scales, b, offs, o
         psum = ctx.enter_context(tc.psum_pool(name="psum", bufs=1))
 
         offsets = keep.tile([P, LEVELS * V // 16], U16, name="offsets")
-        tables = [keep.tile([P, T], F32, name=f"table{l}") for l in range(LEVELS)]
+        table01 = keep.tile([P, 2, T], F32, name="table01")
+        table2 = keep.tile([P, T], F32, name="table2")
+        table3 = keep.tile([P, T], F32, name="table3")
+        tables = [table01[:, 0, :], table01[:, 1, :], table2[:], table3[:]]
+        trigger = keep.tile([P, P], F32, name="trigger")
         w_codes = keep.tile([P, M], U32, name="w_codes", align_bytes=64)
         w_plane = keep.tile([P, M], U8, name="w_plane", align_bytes=64)
         bias_rows = keep.tile([P, P], F32, name="bias_rows")
@@ -49,14 +52,12 @@ def tile_picked_grid_lin_bias_sub_l_kernel(tc, xT, w_words, w_scales, b, offs, o
         make_identity(nc, ident[:])
 
         l3 = LEVELS - 1
-        x_levels = xT.rearrange("(f l) t -> l f t", l=LEVELS)
-        nc.sync.dma_start(tables[0][:], x_levels[0])
+        x_rows = xT.rearrange("(f l) t -> f l t", l=LEVELS)
+        nc.sync.dma_start(table01[:], x_rows[:, 0:2, :])
         nc.sync.dma_start(offsets[:], offs)
         nc.sync.dma_start(bias_rows[0 : M // P, :], b.rearrange("(j p) o -> j (p o)", p=P))
-        for l in range(1, l3):
-            nc.sync.dma_start(tables[l][:], x_levels[l])
-        nc.sync.dma_start(tables[l3][:, :SPLIT], x_levels[l3][:, :SPLIT])
-        nc.sync.dma_start(tables[l3][:, SPLIT:], x_levels[l3][:, SPLIT:])
+        nc.sync.dma_start(table2[:], x_rows[:, 2, :])
+        nc.sync.dma_start(table3[:], x_rows[:, 3, :])
         for q in range(4):
             nc.sync.dma_start(w_plane[32 * q : 32 * q + 4, :].bitcast(I32), w_scales[0, 4 * q : 4 * q + 4, :].bitcast(I32))
         nc.sync.dma_start(w_codes[:].bitcast(I32), w_words[0].rearrange("p m t -> p (m t)").bitcast(I32))
@@ -64,16 +65,17 @@ def tile_picked_grid_lin_bias_sub_l_kernel(tc, xT, w_words, w_scales, b, offs, o
         turned = psum.tile([P, P], F32, name="turned", tag="bank7")
         nc.tensor.transpose(turned[:], bias_rows[:], ident[:])
         nc.scalar.activation(bias[:], turned[:, 0 : M // P], IDENT)
-        for i in range(WARM):
-            nc.tensor.transpose(turned[:], tables[l3][:, 0:P], ident[:])
 
         cols = V // 16
         for l in range(l3):
-            nc.vector.tensor_copy(xb[:, :, l], tables[l][:].indirect(offsets[:, l * cols : (l + 1) * cols]))
+            nc.vector.tensor_copy(xb[:, :, l], tables[l].indirect(offsets[:, l * cols : (l + 1) * cols]))
+        nc.vector.tensor_copy(trigger[:], xb[:, 0:P, l3 - 1])
+        for i in range(WARM):
+            nc.tensor.transpose(turned[:], trigger[:], ident[:])
 
         def gather(n):
             c0 = l3 * cols + n * (G // 16)
-            nc.vector.tensor_tensor(last[:, n * G : (n + 1) * G], tables[l3][:].indirect(offsets[:, c0 : c0 + G // 16]), ones[:], MULT)
+            nc.vector.tensor_tensor(last[:, n * G : (n + 1) * G], tables[l3].indirect(offsets[:, c0 : c0 + G // 16]), ones[:], MULT)
 
         def cast(n, on_vector):
             vs = slice(n * G, (n + 1) * G)
@@ -134,9 +136,9 @@ def tile_picked_grid_lin_bias_sub_l_kernel(tc, xT, w_words, w_scales, b, offs, o
         quant(2)
         quant(3)
         product(0, (0, 1))
-        product(1, (2,))
-        product(2, (3,))
-        product(3, (4, 5, 6, 7))
+        product(1, (2, 3))
+        product(2, (4, 5))
+        product(3, (6, 7))
         empty(0, 0, False)
         empty(0, 1, False)
         store(0, 2, 0, G)
@@ -145,17 +147,15 @@ def tile_picked_grid_lin_bias_sub_l_kernel(tc, xT, w_words, w_scales, b, offs, o
         store(2, 4, 0, G)
         empty(1, 0, False)
         empty(1, 1, False)
-        empty(1, 2, False)
-        empty(1, 3, False)
-        empty(2, 0, True)
-        empty(2, 1, True)
+        empty(1, 2, True)
+        empty(1, 3, True)
+        store(0, 4, G, 2 * G)
+        empty(2, 0, False)
+        empty(2, 1, False)
         empty(2, 2, True)
         empty(2, 3, True)
         empty(3, 0, False)
-        store(0, 1, G, V)
         empty(3, 1, False)
-        store(1, 2, G, V)
-        empty(3, 2, False)
-        store(2, 3, G, V)
+        empty(3, 2, True)
         empty(3, 3, True)
-        store(3, 4, G, V)
+        store(0, 4, 2 * G, V)

from contextlib import ExitStack

import concourse.mybir as mybir
from concourse.masks import make_identity

K, T, LEVELS, V, M = 512, 4096, 4, 512, 512
P = 128
FLOPS = 2 * K * V * M

F32 = mybir.dt.float32
BF16 = mybir.dt.bfloat16
I32 = mybir.dt.int32
U32 = mybir.dt.uint32
U16 = mybir.dt.uint16
U8 = mybir.dt.uint8
FP8X4 = mybir.dt.float8_e4m3fn_x4
MULT = mybir.AluOpType.mult
ADD = mybir.AluOpType.add
IDENT = mybir.ActivationFunctionType.Identity

G = 128
WARM = 20


def tile_picked_grid_lin_bias_sub_l_kernel(tc, xT, w_words, w_scales, b, offs, out):
    nc = tc.nc
    with ExitStack() as ctx:
        keep = ctx.enter_context(tc.tile_pool(name="keep", bufs=1))
        psum = ctx.enter_context(tc.psum_pool(name="psum", bufs=1))

        offsets = keep.tile([P, LEVELS * V // 16], U16, name="offsets")
        table01 = keep.tile([P, 2, T], F32, name="table01")
        table2 = keep.tile([P, T], F32, name="table2")
        table3 = keep.tile([P, T], F32, name="table3")
        tables = [table01[:, 0, :], table01[:, 1, :], table2[:], table3[:]]
        trigger = keep.tile([P, P], F32, name="trigger")
        w_codes = keep.tile([P, M], U32, name="w_codes", align_bytes=64)
        w_plane = keep.tile([P, M], U8, name="w_plane", align_bytes=64)
        bias_rows = keep.tile([P, P], F32, name="bias_rows")
        ident = keep.tile([P, P], F32, name="ident")
        bias = keep.tile([P, M // P], F32, name="bias")
        ones = keep.tile([P, G], F32, name="ones")
        last = keep.tile([P, V], F32, name="last")
        xb = keep.tile([P, V, LEVELS], BF16, name="xb", align_bytes=64)
        x_codes = keep.tile([P, V], U32, name="x_codes", align_bytes=64)
        x_plane = keep.tile([P, V], U8, name="x_plane", align_bytes=64)
        res = keep.tile([P, M // P, V], F32, name="res")

        nc.vector.memset(bias_rows[:], 0.0)
        nc.vector.memset(w_plane[:].bitcast(I32), 0)
        nc.vector.memset(ones[:], 1.0)
        make_identity(nc, ident[:])

        l3 = LEVELS - 1
        x_rows = xT.rearrange("(f l) t -> f l t", l=LEVELS)
        nc.sync.dma_start(table01[:], x_rows[:, 0:2, :])
        nc.sync.dma_start(offsets[:], offs)
        nc.sync.dma_start(bias_rows[0 : M // P, :], b.rearrange("(j p) o -> j (p o)", p=P))
        nc.sync.dma_start(table2[:], x_rows[:, 2, :])
        nc.sync.dma_start(table3[:], x_rows[:, 3, :])
        for q in range(4):
            nc.sync.dma_start(w_plane[32 * q : 32 * q + 4, :].bitcast(I32), w_scales[0, 4 * q : 4 * q + 4, :].bitcast(I32))
        nc.sync.dma_start(w_codes[:].bitcast(I32), w_words[0].rearrange("p m t -> p (m t)").bitcast(I32))

        turned = psum.tile([P, P], F32, name="turned", tag="bank7")
        nc.tensor.transpose(turned[:], bias_rows[:], ident[:])
        nc.scalar.activation(bias[:], turned[:, 0 : M // P], IDENT)

        cols = V // 16
        for l in range(l3):
            nc.vector.tensor_copy(xb[:, :, l], tables[l].indirect(offsets[:, l * cols : (l + 1) * cols]))
        nc.vector.tensor_copy(trigger[:], xb[:, 0:P, l3 - 1])
        for i in range(WARM):
            nc.tensor.transpose(turned[:], trigger[:], ident[:])

        def gather(n):
            c0 = l3 * cols + n * (G // 16)
            nc.vector.tensor_tensor(last[:, n * G : (n + 1) * G], tables[l3].indirect(offsets[:, c0 : c0 + G // 16]), ones[:], MULT)

        def cast(n, on_vector):
            vs = slice(n * G, (n + 1) * G)
            if on_vector:
                nc.vector.tensor_copy(xb[:, vs, l3], last[:, vs])
            else:
                nc.scalar.activation(xb[:, vs, l3], last[:, vs], IDENT)

        def quant(n):
            vs = slice(n * G, (n + 1) * G)
            nc.vector.quantize_mx(
                out=x_codes[:, vs].bitcast(FP8X4),
                scales=x_plane[:, vs],
                in_=xb[:, vs, :].rearrange("p v l -> p (v l)"),
            )

        out_v = out.rearrange("(j p) v -> p j v", p=P)
        accs = {}

        def product(n, banks):
            vs = slice(n * G, (n + 1) * G)
            per_bank = 4 // len(banks)
            for h, bank in enumerate(banks):
                acc = psum.tile([P, per_bank, G], F32, name=f"acc{bank}", tag=f"bank{bank}")
                for i in range(per_bank):
                    j = h * per_bank + i
                    accs[(n, j)] = acc[:, i, :]
                    nc.tensor.matmul_mx(
                        out=acc[:, i, :],
                        lhsT=w_codes[:, j * P : (j + 1) * P].bitcast(FP8X4),
                        lhsT_scale=w_plane[:, j * P : (j + 1) * P],
                        rhs=x_codes[:, vs].bitcast(FP8X4),
                        rhs_scale=x_plane[:, vs],
                        start=True,
                        stop=True,
                    )

        def empty(n, j, on_vector):
            vs = slice(n * G, (n + 1) * G)
            if on_vector:
                nc.vector.tensor_scalar(res[:, j, vs], accs[(n, j)], bias[:, j : j + 1], None, ADD)
            else:
                nc.scalar.activation(res[:, j, vs], accs[(n, j)], IDENT, bias=bias[:, j : j + 1])

        def store(j0, j1, v0, v1):
            nc.sync.dma_start(out_v[:, j0:j1, v0:v1], res[:, j0:j1, v0:v1])

        gather(0)
        gather(1)
        cast(0, True)
        cast(1, False)
        gather(2)
        quant(0)
        cast(2, False)
        gather(3)
        quant(1)
        cast(3, True)
        quant(2)
        quant(3)
        product(0, (0, 1))
        product(1, (2, 3))
        product(2, (4, 5))
        product(3, (6, 7))
        empty(0, 0, False)
        empty(0, 1, False)
        store(0, 2, 0, G)
        empty(0, 2, False)
        empty(0, 3, False)
        store(2, 4, 0, G)
        empty(1, 0, False)
        empty(1, 1, False)
        empty(1, 2, True)
        empty(1, 3, True)
        store(0, 4, G, 2 * G)
        empty(2, 0, False)
        empty(2, 1, False)
        empty(2, 2, True)
        empty(2, 3, True)
        empty(3, 0, False)
        empty(3, 1, False)
        empty(3, 2, True)
        empty(3, 3, True)
        store(0, 4, 2 * G, V)
